import numpy as np
import ml_dtypes


def mxq(x, axis, fmt="e4m3"):
    dtype, down = {"e4m3": (ml_dtypes.float8_e4m3fn, 7), "e5m2": (ml_dtypes.float8_e5m2, 14)}[fmt]
    v = np.moveaxis(np.asarray(x, np.float32).astype(ml_dtypes.bfloat16).astype(np.float64), axis, -1)
    blocks = v.reshape(v.shape[:-1] + (-1, 32))
    amax = np.abs(blocks).max(-1, keepdims=True)
    byte = np.maximum(np.where(amax > 0, np.frexp(amax)[1] - 1 + 127, 0) - down, 1)
    scale = np.exp2(byte - 127.0)
    codes = (blocks / scale).astype(np.float32).astype(dtype).astype(np.float64)
    return np.moveaxis((codes * scale).reshape(v.shape), -1, axis)


WIDE = False


def mx_kscale(k):
    if not WIDE:
        return np.ones(k)
    levels = np.array([10, -10, 5, -5, 0])
    if k % 512:
        return np.exp2(np.random.permutation(np.resize(levels, k // 32))).repeat(32)
    a = np.empty((k // 512, 16))
    for p in range(k // 512):
        a[p, :8] = np.random.permutation(np.resize(levels, 8))
        for g in range(8):
            far = levels[np.abs(levels - a[p, g]) >= 10]
            a[p, g + 8] = far[np.random.randint(len(far))]
    return np.exp2(a.ravel()).repeat(32)


def f64(x):
    return np.asarray(x).astype(np.float64)


def striped(idx):
    return np.tile(idx.reshape(-1, 16).T, (8, 1)).astype(np.uint16)


def unstriped(offs):
    return offs[:16].T.reshape(-1).astype(np.int64)


K, T, E, C, N = 128, 512, 12, 128, 512
TOP = 3


def by_expert(wq, xq):
    return np.concatenate([wq[e].T @ xq[:, e * C:(e + 1) * C] for e in range(E)], axis=1)


def setup_inputs():
    n = np.random.standard_normal
    s = mx_kscale(N)[:, None]
    deal = np.repeat(np.arange(E), C).reshape(TOP, T)[:, np.random.permutation(T)]
    deal = np.take_along_axis(deal, np.argsort(np.random.rand(TOP, T), axis=0), axis=0)
    for _ in range(8):
        s_, t_ = np.random.permutation(T).reshape(2, -1); r = np.random.randint(TOP, size=T // 2); x, y = deal[r, s_].copy(), deal[r, t_].copy()
        ok = ~((deal[:, s_] == y).any(0) | (deal[:, t_] == x).any(0)); deal[r[ok], s_[ok]] = y[ok]; deal[r[ok], t_[ok]] = x[ok]
    order = np.lexsort((np.random.rand(TOP * T), deal.reshape(-1)))
    slot_token = order % T; pos = np.empty(TOP * T, np.int64); pos[order] = np.arange(TOP * T); pos = pos.reshape(TOP, T)
    g = np.random.uniform(0.5, 1.5, (TOP, T)); g = g / g.sum(0)
    w_slot = np.empty(E * C)
    for r in range(TOP): w_slot[pos[r]] = g[r]
    return {
        "dyT": (n((N, T)) * s).astype(np.float32),
        "w": (n((E + 1, N, K)) / np.sqrt(N) / s[None]).astype(np.float32),
        "gate": np.tile(w_slot, (N, 1)).astype(np.float32),
        "offs": striped(slot_token),
        "pos1": striped(pos[0]),
        "pos2": striped(pos[1]),
        "pos3": striped(pos[2]),
    }


def reference(dyT, w, gate, offs, pos1, pos2, pos3):
    idx = unstriped(offs)
    gq = mxq(f64(gate) * f64(dyT)[:, idx], 0, "e4m3")
    wq = mxq(f64(w), 1, "e4m3")
    ds = wq[E].T @ mxq(f64(dyT), 0, "e4m3")
    dx = by_expert(wq, gq)
    return ds + dx[:, unstriped(pos1)] + dx[:, unstriped(pos2)] + dx[:, unstriped(pos3)]

@@ -1,0 +1,211 @@
+from contextlib import ExitStack
+
+import concourse.mybir as mybir
+
+K, T, E, C, N = 128, 512, 12, 128, 512
+SLOTS = E * C
+P = 128
+PACK = 4
+PAIR = 2
+PER_COLUMN = 16
+
+F32 = mybir.dt.float32
+BF16 = mybir.dt.bfloat16
+U32 = mybir.dt.uint32
+U16 = mybir.dt.uint16
+U8 = mybir.dt.uint8
+FP8X4 = mybir.dt.float8_e4m3fn_x4
+MULT = mybir.AluOpType.mult
+ADD = mybir.AluOpType.add
+
+CHUNKS = [(0, 3), (3, 3), (6, 3), (9, 2), (11, 1)]
+TOKEN_PARTS = [(0, 320), (320, 192)]
+HALF = T // 2
+
+FLOPS = 2 * N * K * (SLOTS + T)
+BYTES = 4 * (N * T + (E + 1) * N * K + SLOTS + K * T) + 2 * P * (SLOTS + 3 * T) // PER_COLUMN
+
+
+def interleave(copy, grouped, planes):
+    copy(
+        grouped.rearrange("p (c i) t -> p c t i", i=PAIR),
+        planes.rearrange("p t (c i) -> p c t i", i=PAIR),
+    )
+
+
+def quantize(nc, codes, scales, grouped, columns):
+    start = 0
+    while start < columns:
+        width = 256 if columns - start >= 256 else 128
+        cols = slice(start, start + width)
+        nc.vector.quantize_mx(
+            out=codes[:, cols].bitcast(FP8X4),
+            scales=scales[:, cols],
+            in_=grouped[:, cols, :].rearrange("p c t -> p (c t)"),
+        )
+        start += width
+
+
+def tile_moe_bds_lin_none_kernel(tc, dyT, w, gate, offs, pos1, pos2, pos3, out):
+    nc = tc.nc
+    with ExitStack() as ctx:
+        keep = ctx.enter_context(tc.tile_pool(name="keep", bufs=1))
+        psum = ctx.enter_context(tc.psum_pool(name="psum", bufs=1))
+
+        dy_rows = dyT.rearrange("(p t) x -> p t x", t=PACK)
+        gate_rows = gate.rearrange("(p t) s -> p t s", t=PACK)
+        w_rows = w.rearrange("e (p t) k -> e p t k", t=PACK)
+
+        offs_sb = keep.tile([P, SLOTS // PER_COLUMN], U16, name="offs_sb")
+        pos_sb = [keep.tile([P, T // PER_COLUMN], U16, name="pos_sb%d" % r) for r in range(3)]
+        dy_plane = [keep.tile([P, T], F32, name="dy_plane%d" % t) for t in range(PACK)]
+        dy_half = [keep.tile([P, PACK, HALF], F32, name="dy_half%d" % h) for h in range(2)]
+        gate_sb = [keep.tile([P, n * C], F32, name="gate_sb%d" % i) for i, (e0, n) in enumerate(CHUNKS)]
+        w_raw = [keep.tile([P, PACK, K], F32, name="w_raw%d" % e) for e in range(E + 1)]
+
+        def load_gate(i):
+            e0, n = CHUNKS[i]
+            nc.sync.dma_start(gate_sb[i][:], gate_rows[:, 0, e0 * C : (e0 + n) * C])
+
+        def load_plane(t):
+            nc.sync.dma_start(dy_plane[t][:], dy_rows[:, t, :])
+
+        def load_w(e):
+            nc.sync.dma_start(w_raw[e][:], w_rows[e])
+
+        def load_half(h):
+            nc.sync.dma_start(dy_half[h][:], dy_rows[:, :, h * HALF : (h + 1) * HALF])
+
+        nc.sync.dma_start(offs_sb[:], offs)
+        load_gate(0)
+        load_plane(0)
+        load_plane(1)
+        load_w(0)
+        load_plane(2)
+        load_w(1)
+        load_plane(3)
+        load_gate(1)
+        for e in (2, 3, 4, 5):
+            load_w(e)
+        load_gate(2)
+        for e in (6, 7, 8):
+            load_w(e)
+        load_gate(3)
+        load_gate(4)
+        for e in (9, 10, 11, 12):
+            load_w(e)
+        load_half(0)
+        load_half(1)
+        for r, pos in enumerate((pos1, pos2, pos3)):
+            nc.sync.dma_start(pos_sb[r][:], pos)
+
+        def operand(name, columns):
+            grouped = keep.tile([P, columns, PACK], BF16, name=name + "_bf16", align_bytes=64)
+            codes = keep.tile([P, columns], U32, name=name + "_codes", align_bytes=64)
+            scales = keep.tile([P, columns], U8, name=name + "_scales", align_bytes=64)
+            return grouped, codes, scales
+
+        g32 = [keep.tile([P, PACK, n * C], F32, name="g32_%d" % i) for i, (e0, n) in enumerate(CHUNKS)]
+        g_op = [operand("g%d" % i, n * C) for i, (e0, n) in enumerate(CHUNKS)]
+        w_op = [operand("w%d" % i, n * K) for i, (e0, n) in enumerate(CHUNKS)]
+        ws_op = operand("ws", K)
+        dy_op = [operand("dy%d" % h, HALF) for h in range(2)]
+        dx_ps = [psum.tile([K, n * C], F32, name="dx_ps%d" % i) for i, (e0, n) in enumerate(CHUNKS)]
+        ds_ps = psum.tile([K, T], F32, name="ds_ps")
+        dx = keep.tile([K, SLOTS], F32, name="dx")
+
+        def gather(i):
+            e0, n = CHUNKS[i]
+            lists = offs_sb[:, e0 * C // PER_COLUMN : (e0 + n) * C // PER_COLUMN]
+            for t in range(PACK):
+                nc.vector.tensor_tensor(g32[i][:, t, :], dy_plane[t][:].indirect(lists), gate_sb[i][:], MULT)
+
+        def round_w(i):
+            e0, n = CHUNKS[i]
+            for j in range(n):
+                interleave(nc.scalar.copy, w_op[i][0][:, j * K : (j + 1) * K, :], w_raw[e0 + j][:])
+
+        def round_g(i):
+            interleave(nc.scalar.copy, g_op[i][0][:], g32[i][:])
+
+        def quantize_op(op, columns):
+            quantize(nc, op[1], op[2], op[0], columns)
+
+        def mm(acc, lhs, lhs_cols, rhs, rhs_cols):
+            nc.tensor.matmul_mx(
+                out=acc,
+                lhsT=lhs[1][:, lhs_cols].bitcast(FP8X4),
+                lhsT_scale=lhs[2][:, lhs_cols],
+                rhs=rhs[1][:, rhs_cols].bitcast(FP8X4),
+                rhs_scale=rhs[2][:, rhs_cols],
+                start=True,
+                stop=True,
+            )
+
+        def multiply(i):
+            e0, n = CHUNKS[i]
+            for j in range(n):
+                cols = slice(j * C, (j + 1) * C)
+                mm(dx_ps[i][:, cols], w_op[i], cols, g_op[i], cols)
+
+        def evacuate(i):
+            e0, n = CHUNKS[i]
+            nc.scalar.copy(dx[:, e0 * C : (e0 + n) * C], dx_ps[i][:])
+
+        last = len(CHUNKS) - 1
+        round_w(0)
+        gather(0)
+        for i in range(last):
+            round_g(i)
+            round_w(i + 1)
+            gather(i + 1)
+            quantize_op(w_op[i], CHUNKS[i][1] * K)
+            quantize_op(g_op[i], CHUNKS[i][1] * C)
+            multiply(i)
+            if i == last - 2:
+                interleave(nc.scalar.copy, ws_op[0][:], w_raw[E][:])
+                interleave(nc.scalar.copy, dy_op[0][0][:], dy_half[0][:])
+            if i > 0:
+                evacuate(i - 1)
+        round_g(last)
+        evacuate(last - 1)
+        quantize_op(w_op[last], K)
+        quantize_op(g_op[last], C)
+        multiply(last)
+        evacuate(last)
+
+        interleave(nc.vector.tensor_copy, dy_op[1][0][:], dy_half[1][:])
+        quantize_op(ws_op, K)
+        for h in range(2):
+            quantize_op(dy_op[h], HALF)
+            mm(ds_ps[:, h * HALF : (h + 1) * HALF], ws_op, slice(0, K), dy_op[h], slice(0, HALF))
+
+        picked = {}
+        sums = {}
+
+        def pick(a, r):
+            t0, n = TOKEN_PARTS[a]
+            picked[a, r] = keep.tile([K, n], F32, name="picked%d_%d" % (a, r))
+            lists = pos_sb[r][:, t0 // PER_COLUMN : (t0 + n) // PER_COLUMN]
+            nc.vector.tensor_copy(picked[a, r][:], dx[:].indirect(lists))
+
+        def add(a, r):
+            t0, n = TOKEN_PARTS[a]
+            before = ds_ps[:, t0 : t0 + n] if r == 0 else sums[a, r - 1][:]
+            sums[a, r] = keep.tile([K, n], F32, name="sum%d_%d" % (a, r))
+            nc.vector.tensor_tensor(sums[a, r][:], picked[a, r][:], before, ADD)
+            if r == 2:
+                nc.sync.dma_start(out[:, t0 : t0 + n], sums[a, r][:])
+
+        pick(0, 0)
+        pick(0, 1)
+        add(0, 0)
+        pick(0, 2)
+        add(0, 1)
+        pick(1, 0)
+        add(0, 2)
+        pick(1, 1)
+        add(1, 0)
+        pick(1, 2)
+        add(1, 1)
+        add(1, 2)

@@ -8,6 +8,7 @@ P = 128
 PACK = 4
 PAIR = 2
 PER_COLUMN = 16
+WINDOW = T + 32
 
 F32 = mybir.dt.float32
 BF16 = mybir.dt.bfloat16
@@ -18,9 +19,8 @@ FP8X4 = mybir.dt.float8_e4m3fn_x4
 MULT = mybir.AluOpType.mult
 ADD = mybir.AluOpType.add
 
-CHUNKS = [(0, 3), (3, 3), (6, 3), (9, 2), (11, 1)]
+CHUNKS = [(0, 4), (4, 4), (8, 3), (11, 1)]
 TOKEN_PARTS = [(0, 320), (320, 192)]
-HALF = T // 2
 
 FLOPS = 2 * N * K * (SLOTS + T)
 BYTES = 4 * (N * T + (E + 1) * N * K + SLOTS + K * T) + 2 * P * (SLOTS + 3 * T) // PER_COLUMN
@@ -31,19 +31,6 @@ def interleave(copy, grouped, planes):
         grouped.rearrange("p (c i) t -> p c t i", i=PAIR),
         planes.rearrange("p t (c i) -> p c t i", i=PAIR),
     )
-
-
-def quantize(nc, codes, scales, grouped, columns):
-    start = 0
-    while start < columns:
-        width = 256 if columns - start >= 256 else 128
-        cols = slice(start, start + width)
-        nc.vector.quantize_mx(
-            out=codes[:, cols].bitcast(FP8X4),
-            scales=scales[:, cols],
-            in_=grouped[:, cols, :].rearrange("p c t -> p (c t)"),
-        )
-        start += width
 
 
 def tile_moe_bds_lin_none_kernel(tc, dyT, w, gate, offs, pos1, pos2, pos3, out):
@@ -58,80 +45,84 @@ def tile_moe_bds_lin_none_kernel(tc, dyT, w, gate, offs, pos1, pos2, pos3, out):
 
         offs_sb = keep.tile([P, SLOTS // PER_COLUMN], U16, name="offs_sb")
         pos_sb = [keep.tile([P, T // PER_COLUMN], U16, name="pos_sb%d" % r) for r in range(3)]
-        dy_plane = [keep.tile([P, T], F32, name="dy_plane%d" % t) for t in range(PACK)]
-        dy_half = [keep.tile([P, PACK, HALF], F32, name="dy_half%d" % h) for h in range(2)]
-        gate_sb = [keep.tile([P, n * C], F32, name="gate_sb%d" % i) for i, (e0, n) in enumerate(CHUNKS)]
+        dy_plane = [keep.tile([P, WINDOW], F32, name="dy_plane%d" % t) for t in range(PACK)]
+        dy_all = keep.tile([P, PACK, T], F32, name="dy_all")
+        gate_sb = keep.tile([P, SLOTS], F32, name="gate_sb")
         w_raw = [keep.tile([P, PACK, K], F32, name="w_raw%d" % e) for e in range(E + 1)]
 
-        def load_gate(i):
-            e0, n = CHUNKS[i]
-            nc.sync.dma_start(gate_sb[i][:], gate_rows[:, 0, e0 * C : (e0 + n) * C])
+        def load_gate(e0, n, queue=nc.sync):
+            cols = slice(e0 * C, (e0 + n) * C)
+            queue.dma_start(gate_sb[:, cols], gate_rows[:, 0, cols])
 
         def load_plane(t):
-            nc.sync.dma_start(dy_plane[t][:], dy_rows[:, t, :])
+            nc.sync.dma_start(dy_plane[t][:, :T], dy_rows[:, t, :])
 
         def load_w(e):
             nc.sync.dma_start(w_raw[e][:], w_rows[e])
 
-        def load_half(h):
-            nc.sync.dma_start(dy_half[h][:], dy_rows[:, :, h * HALF : (h + 1) * HALF])
-
-        nc.sync.dma_start(offs_sb[:], offs)
-        load_gate(0)
         load_plane(0)
+        nc.sync.dma_start(offs_sb[:], offs)
+        load_gate(0, 1, nc.scalar)
+        load_gate(1, 3)
         load_plane(1)
         load_w(0)
         load_plane(2)
         load_w(1)
         load_plane(3)
-        load_gate(1)
-        for e in (2, 3, 4, 5):
+        load_w(2)
+        load_w(3)
+        load_gate(4, 4)
+        for e in (4, 5, 6, 7):
             load_w(e)
-        load_gate(2)
-        for e in (6, 7, 8):
+        load_gate(8, 4)
+        for e in (8, 9, 10, 11, 12):
             load_w(e)
-        load_gate(3)
-        load_gate(4)
-        for e in (9, 10, 11, 12):
-            load_w(e)
-        load_half(0)
-        load_half(1)
+        nc.sync.dma_start(dy_all[:], dy_rows)
         for r, pos in enumerate((pos1, pos2, pos3)):
             nc.sync.dma_start(pos_sb[r][:], pos)
 
-        def operand(name, columns):
-            grouped = keep.tile([P, columns, PACK], BF16, name=name + "_bf16", align_bytes=64)
+        def batch(name, columns, tag=None):
+            grouped = keep.tile([P, columns, PACK], BF16, name=name + "_bf16", tag=tag or name + "_bf16", align_bytes=64)
             codes = keep.tile([P, columns], U32, name=name + "_codes", align_bytes=64)
             scales = keep.tile([P, columns], U8, name=name + "_scales", align_bytes=64)
             return grouped, codes, scales
 
         g32 = [keep.tile([P, PACK, n * C], F32, name="g32_%d" % i) for i, (e0, n) in enumerate(CHUNKS)]
-        g_op = [operand("g%d" % i, n * C) for i, (e0, n) in enumerate(CHUNKS)]
-        w_op = [operand("w%d" % i, n * K) for i, (e0, n) in enumerate(CHUNKS)]
-        ws_op = operand("ws", K)
-        dy_op = [operand("dy%d" % h, HALF) for h in range(2)]
+        g_batch = [batch("g0", 512), batch("g1", 512), batch("g2", 512), batch("g3", 128, "late")]
+        w_batch = [batch("w0", 512), batch("w1", 512), batch("w2", 512)]
+        w_place = {e: (w_batch[e // 4], e % 4) for e in range(11)}
+        w_place[11] = (w_batch[2], 3)
+        w_place[12] = (g_batch[2], 3)
         dx_ps = [psum.tile([K, n * C], F32, name="dx_ps%d" % i) for i, (e0, n) in enumerate(CHUNKS)]
         ds_ps = psum.tile([K, T], F32, name="ds_ps")
         dx = keep.tile([K, SLOTS], F32, name="dx")
 
-        def gather(i):
-            e0, n = CHUNKS[i]
-            lists = offs_sb[:, e0 * C // PER_COLUMN : (e0 + n) * C // PER_COLUMN]
-            for t in range(PACK):
-                nc.vector.tensor_tensor(g32[i][:, t, :], dy_plane[t][:].indirect(lists), gate_sb[i][:], MULT)
+        def gather(i, t, first, count):
+            s0 = CHUNKS[i][0] * C + first
+            lists = offs_sb[:, s0 // PER_COLUMN : (s0 + count) // PER_COLUMN]
+            nc.vector.tensor_tensor(
+                g32[i][:, t, first : first + count], dy_plane[t][:].indirect(lists), gate_sb[:, s0 : s0 + count], MULT
+            )
 
-        def round_w(i):
-            e0, n = CHUNKS[i]
-            for j in range(n):
-                interleave(nc.scalar.copy, w_op[i][0][:, j * K : (j + 1) * K, :], w_raw[e0 + j][:])
+        def gather_chunk(i):
+            for t in range(PACK):
+                gather(i, t, 0, CHUNKS[i][1] * C)
+
+        def round_w(e):
+            op, j = w_place[e]
+            interleave(nc.scalar.copy, op[0][:, j * K : (j + 1) * K, :], w_raw[e][:])
 
         def round_g(i):
-            interleave(nc.scalar.copy, g_op[i][0][:], g32[i][:])
+            interleave(nc.scalar.copy, g_batch[i][0][:, : CHUNKS[i][1] * C, :], g32[i][:])
 
-        def quantize_op(op, columns):
-            quantize(nc, op[1], op[2], op[0], columns)
+        def quantize(op):
+            nc.vector.quantize_mx(
+                out=op[1][:].bitcast(FP8X4), scales=op[2][:], in_=op[0][:].rearrange("p c t -> p (c t)")
+            )
 
-        def mm(acc, lhs, lhs_cols, rhs, rhs_cols):
+        def mm(acc, e, rhs, rhs_cols):
+            lhs, j = w_place[e]
+            lhs_cols = slice(j * K, (j + 1) * K)
             nc.tensor.matmul_mx(
                 out=acc,
                 lhsT=lhs[1][:, lhs_cols].bitcast(FP8X4),
@@ -146,39 +137,49 @@ def tile_moe_bds_lin_none_kernel(tc, dyT, w, gate, offs, pos1, pos2, pos3, out):
             e0, n = CHUNKS[i]
             for j in range(n):
                 cols = slice(j * C, (j + 1) * C)
-                mm(dx_ps[i][:, cols], w_op[i], cols, g_op[i], cols)
+                mm(dx_ps[i][:, cols], e0 + j, g_batch[i], cols)
 
         def evacuate(i):
             e0, n = CHUNKS[i]
             nc.scalar.copy(dx[:, e0 * C : (e0 + n) * C], dx_ps[i][:])
 
-        last = len(CHUNKS) - 1
-        round_w(0)
-        gather(0)
-        for i in range(last):
-            round_g(i)
-            round_w(i + 1)
-            gather(i + 1)
-            quantize_op(w_op[i], CHUNKS[i][1] * K)
-            quantize_op(g_op[i], CHUNKS[i][1] * C)
-            multiply(i)
-            if i == last - 2:
-                interleave(nc.scalar.copy, ws_op[0][:], w_raw[E][:])
-                interleave(nc.scalar.copy, dy_op[0][0][:], dy_half[0][:])
-            if i > 0:
-                evacuate(i - 1)
-        round_g(last)
-        evacuate(last - 1)
-        quantize_op(w_op[last], K)
-        quantize_op(g_op[last], C)
-        multiply(last)
-        evacuate(last)
+        gather(0, 0, 0, C)
+        gather(0, 0, C, 3 * C)
+        for t in range(1, PACK):
+            gather(0, t, 0, 4 * C)
+        for e in range(4):
+            round_w(e)
+        round_g(0)
+        gather_chunk(1)
+        for e in range(4, 8):
+            round_w(e)
+        round_g(1)
+        quantize(w_batch[0])
+        quantize(g_batch[0])
+        multiply(0)
+        gather_chunk(2)
+        for e in range(8, 13):
+            round_w(e)
+        round_g(2)
+        quantize(w_batch[1])
+        quantize(g_batch[1])
+        multiply(1)
+        gather_chunk(3)
+        round_g(3)
+        evacuate(0)
+        evacuate(1)
+        quantize(w_batch[2])
+        quantize(g_batch[2])
+        multiply(2)
+        quantize(g_batch[3])
+        multiply(3)
+        evacuate(2)
+        evacuate(3)
 
-        interleave(nc.vector.tensor_copy, dy_op[1][0][:], dy_half[1][:])
-        quantize_op(ws_op, K)
-        for h in range(2):
-            quantize_op(dy_op[h], HALF)
-            mm(ds_ps[:, h * HALF : (h + 1) * HALF], ws_op, slice(0, K), dy_op[h], slice(0, HALF))
+        dy_batch = batch("dy", T, "late")
+        interleave(nc.vector.tensor_copy, dy_batch[0][:], dy_all[:])
+        quantize(dy_batch)
+        mm(ds_ps[:], E, dy_batch, slice(0, T))
 
         picked = {}
         sums = {}
@@ -189,23 +190,23 @@ def tile_moe_bds_lin_none_kernel(tc, dyT, w, gate, offs, pos1, pos2, pos3, out):
             lists = pos_sb[r][:, t0 // PER_COLUMN : (t0 + n) // PER_COLUMN]
             nc.vector.tensor_copy(picked[a, r][:], dx[:].indirect(lists))
 
-        def add(a, r):
+        def add(a, r, engine):
             t0, n = TOKEN_PARTS[a]
             before = ds_ps[:, t0 : t0 + n] if r == 0 else sums[a, r - 1][:]
             sums[a, r] = keep.tile([K, n], F32, name="sum%d_%d" % (a, r))
-            nc.vector.tensor_tensor(sums[a, r][:], picked[a, r][:], before, ADD)
+            engine.tensor_tensor(sums[a, r][:], picked[a, r][:], before, ADD)
             if r == 2:
                 nc.sync.dma_start(out[:, t0 : t0 + n], sums[a, r][:])
 
         pick(0, 0)
         pick(0, 1)
-        add(0, 0)
+        add(0, 0, nc.vector)
         pick(0, 2)
-        add(0, 1)
+        add(0, 1, nc.vector)
         pick(1, 0)
-        add(0, 2)
+        add(0, 2, nc.vector)
         pick(1, 1)
-        add(1, 0)
+        add(1, 0, nc.vector)
         pick(1, 2)
-        add(1, 1)
-        add(1, 2)
+        add(1, 1, nc.vector)
+        add(1, 2, nc.vector)

@@ -9,6 +9,7 @@ PACK = 4
 PAIR = 2
 PER_COLUMN = 16
 WINDOW = T + 32
+SHARED = E
 
 F32 = mybir.dt.float32
 BF16 = mybir.dt.bfloat16
@@ -19,8 +20,9 @@ FP8X4 = mybir.dt.float8_e4m3fn_x4
 MULT = mybir.AluOpType.mult
 ADD = mybir.AluOpType.add
 
-CHUNKS = [(0, 4), (4, 4), (8, 3), (11, 1)]
-TOKEN_PARTS = [(0, 320), (320, 192)]
+CHUNKS = [(0, 4), (4, 4), (8, 4)]
+FIRST = 320
+LAST = T - FIRST
 
 FLOPS = 2 * N * K * (SLOTS + T)
 BYTES = 4 * (N * T + (E + 1) * N * K + SLOTS + K * T) + 2 * P * (SLOTS + 3 * T) // PER_COLUMN
@@ -50,7 +52,7 @@ def tile_moe_bds_lin_none_kernel(tc, dyT, w, gate, offs, pos1, pos2, pos3, out):
         gate_sb = keep.tile([P, SLOTS], F32, name="gate_sb")
         w_raw = [keep.tile([P, PACK, K], F32, name="w_raw%d" % e) for e in range(E + 1)]
 
-        def load_gate(e0, n, queue=nc.sync):
+        def load_gate(e0, n, queue):
             cols = slice(e0 * C, (e0 + n) * C)
             queue.dma_start(gate_sb[:, cols], gate_rows[:, 0, cols])
 
@@ -63,7 +65,7 @@ def tile_moe_bds_lin_none_kernel(tc, dyT, w, gate, offs, pos1, pos2, pos3, out):
         load_plane(0)
         nc.sync.dma_start(offs_sb[:], offs)
         load_gate(0, 1, nc.scalar)
-        load_gate(1, 3)
+        load_gate(1, 3, nc.sync)
         load_plane(1)
         load_w(0)
         load_plane(2)
@@ -71,31 +73,47 @@ def tile_moe_bds_lin_none_kernel(tc, dyT, w, gate, offs, pos1, pos2, pos3, out):
         load_plane(3)
         load_w(2)
         load_w(3)
-        load_gate(4, 4)
-        for e in (4, 5, 6, 7):
-            load_w(e)
-        load_gate(8, 4)
-        for e in (8, 9, 10, 11, 12):
+        load_gate(4, 4, nc.sync)
+        load_w(4)
+        load_gate(8, 4, nc.sync)
+        for e in range(5, 13):
             load_w(e)
         nc.sync.dma_start(dy_all[:], dy_rows)
         for r, pos in enumerate((pos1, pos2, pos3)):
             nc.sync.dma_start(pos_sb[r][:], pos)
 
-        def batch(name, columns, tag=None):
-            grouped = keep.tile([P, columns, PACK], BF16, name=name + "_bf16", tag=tag or name + "_bf16", align_bytes=64)
-            codes = keep.tile([P, columns], U32, name=name + "_codes", align_bytes=64)
-            scales = keep.tile([P, columns], U8, name=name + "_scales", align_bytes=64)
-            return grouped, codes, scales
+        def rounded(name, blocks, tag=None):
+            return keep.tile([P, blocks * C, PACK], BF16, name=name, tag=tag or name, align_bytes=64)
+
+        operand = {}
+
+        def quantize(name, source, keys, codes_tag=None, scales_tag=None):
+            columns = len(keys) * C
+            codes = keep.tile([P, columns], U32, name=name + "_codes", tag=codes_tag or name + "_codes", align_bytes=64)
+            scales = keep.tile([P, columns], U8, name=name + "_scales", tag=scales_tag or name + "_scales", align_bytes=64)
+            nc.vector.quantize_mx(
+                out=codes[:].bitcast(FP8X4), scales=scales[:], in_=source.rearrange("p c t -> p (c t)")
+            )
+            for j, key in enumerate(keys):
+                operand[key] = (codes, scales, j * C)
+
+        def matmul(acc, e, key, columns):
+            w_codes, w_scales, w0 = operand["w", e]
+            codes, scales, c0 = operand[key]
+            nc.tensor.matmul_mx(
+                out=acc,
+                lhsT=w_codes[:, w0 : w0 + K].bitcast(FP8X4),
+                lhsT_scale=w_scales[:, w0 : w0 + K],
+                rhs=codes[:, c0 : c0 + columns].bitcast(FP8X4),
+                rhs_scale=scales[:, c0 : c0 + columns],
+                start=True,
+                stop=True,
+            )
 
         g32 = [keep.tile([P, PACK, n * C], F32, name="g32_%d" % i) for i, (e0, n) in enumerate(CHUNKS)]
-        g_batch = [batch("g0", 512), batch("g1", 512), batch("g2", 512), batch("g3", 128, "late")]
-        w_batch = [batch("w0", 512), batch("w1", 512), batch("w2", 512)]
-        w_place = {e: (w_batch[e // 4], e % 4) for e in range(11)}
-        w_place[11] = (w_batch[2], 3)
-        w_place[12] = (g_batch[2], 3)
-        dx_ps = [psum.tile([K, n * C], F32, name="dx_ps%d" % i) for i, (e0, n) in enumerate(CHUNKS)]
-        ds_ps = psum.tile([K, T], F32, name="ds_ps")
         dx = keep.tile([K, SLOTS], F32, name="dx")
+        ds_ps = psum.tile([K, T], F32, name="ds_ps")
+        dx_ps = {}
 
         def gather(i, t, first, count):
             s0 = CHUNKS[i][0] * C + first
@@ -108,105 +126,95 @@ def tile_moe_bds_lin_none_kernel(tc, dyT, w, gate, offs, pos1, pos2, pos3, out):
             for t in range(PACK):
                 gather(i, t, 0, CHUNKS[i][1] * C)
 
-        def round_w(e):
-            op, j = w_place[e]
-            interleave(nc.scalar.copy, op[0][:, j * K : (j + 1) * K, :], w_raw[e][:])
+        def blocks(tile, j, n=1):
+            return tile[:, j * C : (j + n) * C, :]
 
-        def round_g(i):
-            interleave(nc.scalar.copy, g_batch[i][0][:, : CHUNKS[i][1] * C, :], g32[i][:])
+        def round_w(e, tile, j):
+            interleave(nc.scalar.copy, blocks(tile, j), w_raw[e][:])
 
-        def quantize(op):
-            nc.vector.quantize_mx(
-                out=op[1][:].bitcast(FP8X4), scales=op[2][:], in_=op[0][:].rearrange("p c t -> p (c t)")
-            )
+        def round_g(i, first, n, tile, j):
+            interleave(nc.scalar.copy, blocks(tile, j, n), g32[i][:, :, first * C : (first + n) * C])
 
-        def mm(acc, e, rhs, rhs_cols):
-            lhs, j = w_place[e]
-            lhs_cols = slice(j * K, (j + 1) * K)
-            nc.tensor.matmul_mx(
-                out=acc,
-                lhsT=lhs[1][:, lhs_cols].bitcast(FP8X4),
-                lhsT_scale=lhs[2][:, lhs_cols],
-                rhs=rhs[1][:, rhs_cols].bitcast(FP8X4),
-                rhs_scale=rhs[2][:, rhs_cols],
-                start=True,
-                stop=True,
-            )
-
-        def multiply(i):
-            e0, n = CHUNKS[i]
+        def multiply(e0, n):
+            dx_ps[e0] = psum.tile([K, n * C], F32, name="dx_ps%d" % e0)
             for j in range(n):
-                cols = slice(j * C, (j + 1) * C)
-                mm(dx_ps[i][:, cols], e0 + j, g_batch[i], cols)
+                matmul(dx_ps[e0][:, j * C : (j + 1) * C], e0 + j, ("g", e0 + j), C)
 
-        def evacuate(i):
-            e0, n = CHUNKS[i]
-            nc.scalar.copy(dx[:, e0 * C : (e0 + n) * C], dx_ps[i][:])
+        def evacuate(e0, n):
+            nc.scalar.copy(dx[:, e0 * C : (e0 + n) * C], dx_ps[e0][:])
+
+        w_a, g_a, w_b, g_b = [rounded(name, 4) for name in ("w_a", "g_a", "w_b", "g_b")]
+        mix_x, mix_y, mix_z = rounded("mix_x", 4), rounded("mix_y", 2), rounded("mix_z", 3)
 
         gather(0, 0, 0, C)
         gather(0, 0, C, 3 * C)
         for t in range(1, PACK):
             gather(0, t, 0, 4 * C)
         for e in range(4):
-            round_w(e)
-        round_g(0)
+            round_w(e, w_a, e)
+        round_g(0, 0, 4, g_a, 0)
         gather_chunk(1)
         for e in range(4, 8):
-            round_w(e)
-        round_g(1)
-        quantize(w_batch[0])
-        quantize(g_batch[0])
-        multiply(0)
+            round_w(e, w_b, e - 4)
+        round_g(1, 0, 4, g_b, 0)
         gather_chunk(2)
-        for e in range(8, 13):
-            round_w(e)
-        round_g(2)
-        quantize(w_batch[1])
-        quantize(g_batch[1])
-        multiply(1)
-        gather_chunk(3)
-        round_g(3)
-        evacuate(0)
-        evacuate(1)
-        quantize(w_batch[2])
-        quantize(g_batch[2])
-        multiply(2)
-        quantize(g_batch[3])
-        multiply(3)
-        evacuate(2)
-        evacuate(3)
+        round_w(8, mix_x, 0)
+        round_w(9, mix_x, 1)
+        round_w(10, mix_y, 0)
+        round_w(11, mix_z, 1)
+        round_w(SHARED, mix_z, 0)
+        round_g(2, 0, 2, mix_x, 2)
+        round_g(2, 2, 1, mix_y, 1)
+        round_g(2, 3, 1, mix_z, 2)
+        quantize("w_a", w_a[:], [("w", e) for e in range(4)])
+        quantize("g_a", g_a[:], [("g", e) for e in range(4)])
+        multiply(0, 4)
+        quantize("w_b", w_b[:], [("w", e) for e in range(4, 8)])
+        quantize("g_b", g_b[:], [("g", e) for e in range(4, 8)])
+        multiply(4, 4)
+        evacuate(0, 4)
+        evacuate(4, 4)
+        quantize("mix_x", mix_x[:], [("w", 8), ("w", 9), ("g", 8), ("g", 9)])
+        multiply(8, 2)
+        quantize("mix_y", mix_y[:], [("w", 10), ("g", 10)])
+        multiply(10, 1)
+        quantize("mix_z", blocks(mix_z, 1, 2), [("w", 11), ("g", 11)], "late_codes", "late_scales")
+        multiply(11, 1)
+        evacuate(8, 2)
+        evacuate(10, 1)
+        evacuate(11, 1)
 
-        dy_batch = batch("dy", T, "late")
-        interleave(nc.vector.tensor_copy, dy_batch[0][:], dy_all[:])
-        quantize(dy_batch)
-        mm(ds_ps[:], E, dy_batch, slice(0, T))
+        interleave(nc.vector.tensor_copy, blocks(mix_z, 1), dy_all[:, :, :C])
+        quantize("shared", blocks(mix_z, 0, 2), [("w", SHARED), ("dy", 0)])
+        matmul(ds_ps[:, :C], SHARED, ("dy", 0), C)
+        for j, n, tag in ((1, 2, "late_codes"), (3, 1, "late_scales")):
+            cols = slice(j * C, (j + n) * C)
+            dy_rounded = rounded("dy_rounded%d" % j, n, tag)
+            interleave(nc.scalar.copy, dy_rounded[:], dy_all[:, :, cols])
+            quantize("dy%d" % j, dy_rounded[:], [("dy", j + u) for u in range(n)])
+            matmul(ds_ps[:, cols], SHARED, ("dy", j), n * C)
 
-        picked = {}
-        sums = {}
-
-        def pick(a, r):
-            t0, n = TOKEN_PARTS[a]
-            picked[a, r] = keep.tile([K, n], F32, name="picked%d_%d" % (a, r))
+        def pick(picked, t0, r):
+            n = picked.shape[1]
             lists = pos_sb[r][:, t0 // PER_COLUMN : (t0 + n) // PER_COLUMN]
-            nc.vector.tensor_copy(picked[a, r][:], dx[:].indirect(lists))
+            nc.vector.tensor_copy(picked, dx[:].indirect(lists))
 
-        def add(a, r, engine):
-            t0, n = TOKEN_PARTS[a]
-            before = ds_ps[:, t0 : t0 + n] if r == 0 else sums[a, r - 1][:]
-            sums[a, r] = keep.tile([K, n], F32, name="sum%d_%d" % (a, r))
-            engine.tensor_tensor(sums[a, r][:], picked[a, r][:], before, ADD)
-            if r == 2:
-                nc.sync.dma_start(out[:, t0 : t0 + n], sums[a, r][:])
+        def add(name, x, y, engine=nc.vector):
+            total = keep.tile([K, x.shape[1]], F32, name=name)
+            engine.tensor_tensor(total[:], x, y, ADD)
+            return total[:]
 
-        pick(0, 0)
-        pick(0, 1)
-        add(0, 0, nc.vector)
-        pick(0, 2)
-        add(0, 1, nc.vector)
-        pick(1, 0)
-        add(0, 2, nc.vector)
-        pick(1, 1)
-        add(1, 0, nc.vector)
-        pick(1, 2)
-        add(1, 1, nc.vector)
-        add(1, 2, nc.vector)
+        a = keep.tile([K, 3, FIRST], F32, name="picked_a")
+        b0 = keep.tile([K, LAST], F32, name="picked_b0")
+        b12 = keep.tile([K, 2, LAST], F32, name="picked_b12", tag="late_codes", align_bytes=64)
+        for r in range(3):
+            pick(a[:, r, :], 0, r)
+        a01 = add("a01", a[:, 0, :], a[:, 1, :], nc.gpsimd)
+        pick(b0[:], FIRST, 0)
+        pick(b12[:, 0, :], FIRST, 1)
+        a012 = add("a012", a01, a[:, 2, :])
+        pick(b12[:, 1, :], FIRST, 2)
+        b01 = add("b01", b0[:], b12[:, 0, :])
+        b2s = add("b2s", b12[:, 1, :], ds_ps[:, FIRST:])
+        nc.sync.dma_start(out[:, :FIRST], add("a_out", a012, ds_ps[:, :FIRST]))
+        nc.sync.dma_start(out[:, FIRST:], add("b_out", b01, b2s))

from contextlib import ExitStack

import concourse.mybir as mybir

K, T, E, C, N = 128, 512, 12, 128, 512
SLOTS = E * C
P = 128
PACK = 4
PAIR = 2
PER_COLUMN = 16
WINDOW = T + 32
SHARED = E

F32 = mybir.dt.float32
BF16 = mybir.dt.bfloat16
U32 = mybir.dt.uint32
U16 = mybir.dt.uint16
U8 = mybir.dt.uint8
FP8X4 = mybir.dt.float8_e4m3fn_x4
MULT = mybir.AluOpType.mult
ADD = mybir.AluOpType.add

CHUNKS = [(0, 4), (4, 4), (8, 4)]
FIRST = 320
LAST = T - FIRST

FLOPS = 2 * N * K * (SLOTS + T)
BYTES = 4 * (N * T + (E + 1) * N * K + SLOTS + K * T) + 2 * P * (SLOTS + 3 * T) // PER_COLUMN


def interleave(copy, grouped, planes):
    copy(
        grouped.rearrange("p (c i) t -> p c t i", i=PAIR),
        planes.rearrange("p t (c i) -> p c t i", i=PAIR),
    )


def tile_moe_bds_lin_none_kernel(tc, dyT, w, gate, offs, pos1, pos2, pos3, out):
    nc = tc.nc
    with ExitStack() as ctx:
        keep = ctx.enter_context(tc.tile_pool(name="keep", bufs=1))
        psum = ctx.enter_context(tc.psum_pool(name="psum", bufs=1))

        dy_rows = dyT.rearrange("(p t) x -> p t x", t=PACK)
        gate_rows = gate.rearrange("(p t) s -> p t s", t=PACK)
        w_rows = w.rearrange("e (p t) k -> e p t k", t=PACK)

        offs_sb = keep.tile([P, SLOTS // PER_COLUMN], U16, name="offs_sb")
        pos_sb = [keep.tile([P, T // PER_COLUMN], U16, name="pos_sb%d" % r) for r in range(3)]
        dy_plane = [keep.tile([P, WINDOW], F32, name="dy_plane%d" % t) for t in range(PACK)]
        dy_all = keep.tile([P, PACK, T], F32, name="dy_all")
        gate_sb = keep.tile([P, SLOTS], F32, name="gate_sb")
        w_raw = [keep.tile([P, PACK, K], F32, name="w_raw%d" % e) for e in range(E + 1)]

        def load_gate(e0, n, queue):
            cols = slice(e0 * C, (e0 + n) * C)
            queue.dma_start(gate_sb[:, cols], gate_rows[:, 0, cols])

        def load_plane(t):
            nc.sync.dma_start(dy_plane[t][:, :T], dy_rows[:, t, :])

        def load_w(e):
            nc.sync.dma_start(w_raw[e][:], w_rows[e])

        load_plane(0)
        nc.sync.dma_start(offs_sb[:], offs)
        load_gate(0, 1, nc.scalar)
        load_gate(1, 3, nc.sync)
        load_plane(1)
        load_w(0)
        load_plane(2)
        load_w(1)
        load_plane(3)
        load_w(2)
        load_w(3)
        load_gate(4, 4, nc.sync)
        load_w(4)
        load_gate(8, 4, nc.sync)
        for e in range(5, 13):
            load_w(e)
        nc.sync.dma_start(dy_all[:], dy_rows)
        for r, pos in enumerate((pos1, pos2, pos3)):
            nc.sync.dma_start(pos_sb[r][:], pos)

        def rounded(name, blocks, tag=None):
            return keep.tile([P, blocks * C, PACK], BF16, name=name, tag=tag or name, align_bytes=64)

        operand = {}

        def quantize(name, source, keys, codes_tag=None, scales_tag=None):
            columns = len(keys) * C
            codes = keep.tile([P, columns], U32, name=name + "_codes", tag=codes_tag or name + "_codes", align_bytes=64)
            scales = keep.tile([P, columns], U8, name=name + "_scales", tag=scales_tag or name + "_scales", align_bytes=64)
            nc.vector.quantize_mx(
                out=codes[:].bitcast(FP8X4), scales=scales[:], in_=source.rearrange("p c t -> p (c t)")
            )
            for j, key in enumerate(keys):
                operand[key] = (codes, scales, j * C)

        def matmul(acc, e, key, columns):
            w_codes, w_scales, w0 = operand["w", e]
            codes, scales, c0 = operand[key]
            nc.tensor.matmul_mx(
                out=acc,
                lhsT=w_codes[:, w0 : w0 + K].bitcast(FP8X4),
                lhsT_scale=w_scales[:, w0 : w0 + K],
                rhs=codes[:, c0 : c0 + columns].bitcast(FP8X4),
                rhs_scale=scales[:, c0 : c0 + columns],
                start=True,
                stop=True,
            )

        g32 = [keep.tile([P, PACK, n * C], F32, name="g32_%d" % i) for i, (e0, n) in enumerate(CHUNKS)]
        dx = keep.tile([K, SLOTS], F32, name="dx")
        ds_ps = psum.tile([K, T], F32, name="ds_ps")
        dx_ps = {}

        def gather(i, t, first, count):
            s0 = CHUNKS[i][0] * C + first
            lists = offs_sb[:, s0 // PER_COLUMN : (s0 + count) // PER_COLUMN]
            nc.vector.tensor_tensor(
                g32[i][:, t, first : first + count], dy_plane[t][:].indirect(lists), gate_sb[:, s0 : s0 + count], MULT
            )

        def gather_chunk(i):
            for t in range(PACK):
                gather(i, t, 0, CHUNKS[i][1] * C)

        def blocks(tile, j, n=1):
            return tile[:, j * C : (j + n) * C, :]

        def round_w(e, tile, j):
            interleave(nc.scalar.copy, blocks(tile, j), w_raw[e][:])

        def round_g(i, first, n, tile, j):
            interleave(nc.scalar.copy, blocks(tile, j, n), g32[i][:, :, first * C : (first + n) * C])

        def multiply(e0, n):
            dx_ps[e0] = psum.tile([K, n * C], F32, name="dx_ps%d" % e0)
            for j in range(n):
                matmul(dx_ps[e0][:, j * C : (j + 1) * C], e0 + j, ("g", e0 + j), C)

        def evacuate(e0, n):
            nc.scalar.copy(dx[:, e0 * C : (e0 + n) * C], dx_ps[e0][:])

        w_a, g_a, w_b, g_b = [rounded(name, 4) for name in ("w_a", "g_a", "w_b", "g_b")]
        mix_x, mix_y, mix_z = rounded("mix_x", 4), rounded("mix_y", 2), rounded("mix_z", 3)

        gather(0, 0, 0, C)
        gather(0, 0, C, 3 * C)
        for t in range(1, PACK):
            gather(0, t, 0, 4 * C)
        for e in range(4):
            round_w(e, w_a, e)
        round_g(0, 0, 4, g_a, 0)
        gather_chunk(1)
        for e in range(4, 8):
            round_w(e, w_b, e - 4)
        round_g(1, 0, 4, g_b, 0)
        gather_chunk(2)
        round_w(8, mix_x, 0)
        round_w(9, mix_x, 1)
        round_w(10, mix_y, 0)
        round_w(11, mix_z, 1)
        round_w(SHARED, mix_z, 0)
        round_g(2, 0, 2, mix_x, 2)
        round_g(2, 2, 1, mix_y, 1)
        round_g(2, 3, 1, mix_z, 2)
        quantize("w_a", w_a[:], [("w", e) for e in range(4)])
        quantize("g_a", g_a[:], [("g", e) for e in range(4)])
        multiply(0, 4)
        quantize("w_b", w_b[:], [("w", e) for e in range(4, 8)])
        quantize("g_b", g_b[:], [("g", e) for e in range(4, 8)])
        multiply(4, 4)
        evacuate(0, 4)
        evacuate(4, 4)
        quantize("mix_x", mix_x[:], [("w", 8), ("w", 9), ("g", 8), ("g", 9)])
        multiply(8, 2)
        quantize("mix_y", mix_y[:], [("w", 10), ("g", 10)])
        multiply(10, 1)
        quantize("mix_z", blocks(mix_z, 1, 2), [("w", 11), ("g", 11)], "late_codes", "late_scales")
        multiply(11, 1)
        evacuate(8, 2)
        evacuate(10, 1)
        evacuate(11, 1)

        interleave(nc.vector.tensor_copy, blocks(mix_z, 1), dy_all[:, :, :C])
        quantize("shared", blocks(mix_z, 0, 2), [("w", SHARED), ("dy", 0)])
        matmul(ds_ps[:, :C], SHARED, ("dy", 0), C)
        for j, n, tag in ((1, 2, "late_codes"), (3, 1, "late_scales")):
            cols = slice(j * C, (j + n) * C)
            dy_rounded = rounded("dy_rounded%d" % j, n, tag)
            interleave(nc.scalar.copy, dy_rounded[:], dy_all[:, :, cols])
            quantize("dy%d" % j, dy_rounded[:], [("dy", j + u) for u in range(n)])
            matmul(ds_ps[:, cols], SHARED, ("dy", j), n * C)

        def pick(picked, t0, r):
            n = picked.shape[1]
            lists = pos_sb[r][:, t0 // PER_COLUMN : (t0 + n) // PER_COLUMN]
            nc.vector.tensor_copy(picked, dx[:].indirect(lists))

        def add(name, x, y, engine=nc.vector):
            total = keep.tile([K, x.shape[1]], F32, name=name)
            engine.tensor_tensor(total[:], x, y, ADD)
            return total[:]

        a = keep.tile([K, 3, FIRST], F32, name="picked_a")
        b0 = keep.tile([K, LAST], F32, name="picked_b0")
        b12 = keep.tile([K, 2, LAST], F32, name="picked_b12", tag="late_codes", align_bytes=64)
        for r in range(3):
            pick(a[:, r, :], 0, r)
        a01 = add("a01", a[:, 0, :], a[:, 1, :], nc.gpsimd)
        pick(b0[:], FIRST, 0)
        pick(b12[:, 0, :], FIRST, 1)
        a012 = add("a012", a01, a[:, 2, :])
        pick(b12[:, 1, :], FIRST, 2)
        b01 = add("b01", b0[:], b12[:, 0, :])
        b2s = add("b2s", b12[:, 1, :], ds_ps[:, FIRST:])
        nc.sync.dma_start(out[:, :FIRST], add("a_out", a012, ds_ps[:, :FIRST]))
        nc.sync.dma_start(out[:, FIRST:], add("b_out", b01, b2s))
